import numpy as np
import ml_dtypes


def mxq(x, axis, fmt="e4m3"):
    dtype, down = {"e4m3": (ml_dtypes.float8_e4m3fn, 7), "e5m2": (ml_dtypes.float8_e5m2, 14)}[fmt]
    v = np.moveaxis(np.asarray(x, np.float32).astype(ml_dtypes.bfloat16).astype(np.float64), axis, -1)
    blocks = v.reshape(v.shape[:-1] + (-1, 32))
    amax = np.abs(blocks).max(-1, keepdims=True)
    byte = np.maximum(np.where(amax > 0, np.frexp(amax)[1] - 1 + 127, 0) - down, 1)
    scale = np.exp2(byte - 127.0)
    codes = (blocks / scale).astype(np.float32).astype(dtype).astype(np.float64)
    return np.moveaxis((codes * scale).reshape(v.shape), -1, axis)


WIDE = False


def mx_kscale(k):
    if not WIDE:
        return np.ones(k)
    levels = np.array([10, -10, 5, -5, 0])
    if k % 512:
        return np.exp2(np.random.permutation(np.resize(levels, k // 32))).repeat(32)
    a = np.empty((k // 512, 16))
    for p in range(k // 512):
        a[p, :8] = np.random.permutation(np.resize(levels, 8))
        for g in range(8):
            far = levels[np.abs(levels - a[p, g]) >= 10]
            a[p, g + 8] = far[np.random.randint(len(far))]
    return np.exp2(a.ravel()).repeat(32)


def f64(x):
    return np.asarray(x).astype(np.float64)


def striped(idx):
    return np.tile(np.asarray(idx).reshape(-1, 16).T, (8, 1)).astype(np.uint16)


def unstriped(offs):
    return offs[:16].T.reshape(-1).astype(np.int64)


E2M1 = np.array([0.0, 0.5, 1.0, 1.5, 2.0, 3.0, 4.0, 6.0, -0.0, -0.5, -1.0, -1.5, -2.0, -3.0, -4.0, -6.0])


def pack_weight(w, fmt):
    k, n = w.shape
    w = f64(np.asarray(w, np.float32).astype(ml_dtypes.bfloat16)).reshape(k // 32, 32, n)
    amax = np.abs(w).max(1)
    if fmt == "e4m3":
        byte = np.frexp(amax)[1] - 1 + 127 - 7
    else:
        mant, ex = np.frexp(amax / 6.0)
        byte = np.where(mant > 0.5, ex, ex - 1) + 127
    byte = np.clip(np.where(amax > 0, byte, 1), 1, 254)
    scaled = (w * np.exp2(127.0 - byte)[:, None, :]).reshape(k, n).astype(np.float32)
    by_word = np.ascontiguousarray(scaled.reshape(k // 512, 128, 4, n).transpose(0, 1, 3, 2))
    if fmt == "e4m3":
        words = by_word.astype(ml_dtypes.float8_e4m3fn).view(np.uint8)
    else:
        c = by_word.astype(ml_dtypes.float4_e2m1fn).view(np.uint8) & 0xF
        words = (c[..., 0::2] | (c[..., 1::2] << 4)).reshape(k // 512, 128, 2 * n)
    return np.ascontiguousarray(words), np.ascontiguousarray(byte.astype(np.uint8).reshape(k // 512, 16, n))


def unpack_weight(words, scales, fmt):
    g, _, n = scales.shape
    words = np.ascontiguousarray(words).reshape(g, 128, n, -1)
    if fmt == "e4m3":
        vals = words.view(ml_dtypes.float8_e4m3fn).astype(np.float64)
    else:
        nib = np.empty((g, 128, n, 4), np.uint8)
        nib[..., 0::2] = words & 0xF
        nib[..., 1::2] = words >> 4
        vals = E2M1[nib]
    vals = vals * np.repeat(np.exp2(scales.astype(np.float64) - 127.0), 8, axis=1)[..., None]
    return vals.transpose(0, 1, 3, 2).reshape(g * 512, n)


D, E, T, I, Q = 512, 512, 2048, 512, 128


def setup_inputs():
    n = np.random.standard_normal
    idx = np.random.permutation(T)[:I]
    fd = mx_kscale(D)
    fe = mx_kscale(E)
    keysp = pack_weight(n((D, T)) / fd[:, None], "e2m1")
    valsp = pack_weight(n((E, T)) / fe[:, None], "e2m1")
    return {
        "query": (n((D, Q)) * 1.0 / np.sqrt(D) * fd[:, None]).astype(np.float32),
        "query2": (n((D, Q)) * 1.0 / np.sqrt(D) * fd[:, None]).astype(np.float32),
        "keys_words": keysp[0],
        "keys_scales": keysp[1],
        "prior1": np.tile(np.random.uniform(0.1, 0.9, T), (128, 1)).astype(np.float32),
        "lam": (np.random.uniform(0.7, 1.4, (Q, 1))).astype(np.float32),
        "gout": (n((E, Q)) * 1 / np.sqrt(E) * fe[:, None]).astype(np.float32),
        "vals_words": valsp[0],
        "vals_scales": valsp[1],
        "base": (0.5 * n((Q, I))).astype(np.float32),
        "offs": striped(idx),
    }


def reference(query, query2, keys_words, keys_scales, prior1, lam, gout, vals_words, vals_scales, base, offs):
    idx = unstriped(offs)
    keysu = unpack_weight(keys_words, keys_scales, "e2m1")
    valsu = unpack_weight(vals_words, vals_scales, "e2m1")
    queryq = mxq(f64(query), 0, "e4m3")
    keysidxg = keysu[:, idx]
    a = queryq.T @ keysidxg
    query2q = mxq(f64(query2), 0, "e4m3")
    b = query2q.T @ keysidxg
    ea = np.exp(a) * f64(prior1)[:1][:, idx]
    eb = np.exp(b) * (1.0 - f64(prior1)[:1][:, idx])
    s = np.log(ea + eb) * f64(lam)
    p = np.exp(s - np.max(s, axis=1, keepdims=True))
    goutq = mxq(f64(gout), 0, "e4m3")
    valsidxg = valsu[:, idx]
    c0 = goutq.T @ valsidxg
    dp = c0 / np.sum(p, axis=1, keepdims=True) + np.sum(c0 * p / np.square(np.sum(p, axis=1, keepdims=True)) * (-1.0), axis=1, keepdims=True)
    ds = dp * p
    dea = ds * f64(lam) / (ea + eb)
    da = dea * f64(prior1)[:1][:, idx] * np.exp(a)
    hda = da * 512.0 * 2.0 * 512.0
    hdea = hda * np.exp(a) * f64(prior1)[:1][:, idx]
    hds = hdea / (ea + eb) * f64(lam)
    hdp = hds * p
    hp = hds * dp + np.sum(hdp * c0 / np.square(np.sum(p, axis=1, keepdims=True)) * (-1.0), axis=1, keepdims=True) + np.sum(hdp, axis=1, keepdims=True) * (-1.0) / np.square(np.sum(p, axis=1, keepdims=True)) * c0 + np.sum(np.sum(hdp, axis=1, keepdims=True) * (-1.0) * c0 * p / np.square(np.square(np.sum(p, axis=1, keepdims=True))) * (-1.0), axis=1, keepdims=True) * np.sum(p, axis=1, keepdims=True) * 2.0
    hs = hp * p
    hea = hs * f64(lam) / (ea + eb) - hdea * ds * f64(lam) / np.square(ea + eb)
    ha = hda * dea * f64(prior1)[:1][:, idx] * np.exp(a) + hea * f64(prior1)[:1][:, idx] * np.exp(a)
    y = ha + f64(base)
    return y

@@ -1,0 +1,176 @@
+from contextlib import ExitStack
+
+import concourse.mybir as mybir
+
+D, E, T, I, Q = 512, 512, 2048, 512, 128
+FLOPS = 3 * 2 * D * Q * I
+
+F32 = mybir.dt.float32
+BF16 = mybir.dt.bfloat16
+I32 = mybir.dt.int32
+U32 = mybir.dt.uint32
+U16 = mybir.dt.uint16
+U8 = mybir.dt.uint8
+FP8X4 = mybir.dt.float8_e4m3fn_x4
+FP4X4 = mybir.dt.float4_e2m1fn_x4
+ALU = mybir.AluOpType
+ACT = mybir.ActivationFunctionType
+
+P = 128
+PACK = 4
+PENALTY = 512.0 * 2.0 * 512.0
+HALF = I // 2
+
+
+def tile_attend_gpeitherquestion_soft_kernel(tc, query, query2, keys_words, keys_scales, prior1, lam, gout, vals_words, vals_scales, base, offs, out):
+    nc = tc.nc
+    with ExitStack() as ctx:
+        sb = ctx.enter_context(tc.tile_pool(name="sb", bufs=1))
+        ps = ctx.enter_context(tc.psum_pool(name="ps", bufs=1))
+
+        def wide(name, tag=None):
+            return sb.tile([P, I], F32, name=name, tag=tag or name, align_bytes=64)
+
+        def column(name):
+            return sb.tile([P, 1], F32, name=name)
+
+        def load_words(name, words):
+            pool = sb.tile([P, T], U16, name=name, tag=name, align_bytes=64)
+            nc.sync.dma_start(out=pool[:].bitcast(I32), in_=words[0].bitcast(I32))
+            return pool
+
+        def load_scales(name, scales):
+            pool = sb.tile([P, T], U8, name=name, tag=name, align_bytes=64)
+            nc.vector.memset(pool[:].bitcast(I32), 0)
+            for r in range(PACK):
+                nc.sync.dma_start(out=pool[r:P:32, :].bitcast(I32), in_=scales[0][r:16:PACK, :].bitcast(I32))
+            return pool
+
+        def load_rows(name, rows):
+            raw = sb.tile([P, PACK, Q], F32, name=name, tag=name, align_bytes=64)
+            nc.sync.dma_start(out=raw[:], in_=rows.rearrange("(p j) w -> p j w", j=PACK))
+            return raw
+
+        def rounded(name, raw, on_scalar, tag=None):
+            grouped = sb.tile([P, Q, PACK], BF16, name=name, tag=tag or name, align_bytes=64)
+            dst = grouped[:].rearrange("p (c i) t -> p c t i", i=4)
+            src = raw[:].rearrange("p t (c i) -> p c t i", i=4)
+            if on_scalar:
+                nc.scalar.activation(dst, src, ACT.Copy)
+            else:
+                nc.vector.tensor_copy(dst, src)
+            return grouped
+
+        def quantised(name, grouped):
+            codes = sb.tile([P, Q], U32, name=name + "_codes", align_bytes=64)
+            scales = sb.tile([P, Q], U8, name=name + "_scales", align_bytes=64)
+            nc.vector.quantize_mx(out=codes[:].bitcast(FP8X4), scales=scales[:], in_=grouped[:].rearrange("p w t -> p (w t)"))
+            return codes, scales
+
+        def gathered(name, pool, dtype, tag=None):
+            picked = sb.tile([P, I], dtype, name=name, tag=tag or name, align_bytes=64)
+            nc.vector.tensor_copy(picked[:], pool[:].indirect(offsets[:]))
+            return picked
+
+        def product(name, stationary, words, scales):
+            acc = ps.tile([P, I], F32, name=name)
+            nc.tensor.matmul_mx(out=acc[:], lhsT=stationary[0][:].bitcast(FP8X4), lhsT_scale=stationary[1][:],
+                                rhs=words[:].bitcast(FP4X4), rhs_scale=scales[:], start=True, stop=True)
+            return acc
+
+        offsets = sb.tile([P, I // 16], U16, name="offsets")
+        nc.sync.dma_start(offsets[:], offs)
+        kw_pool = load_words("kw_pool", keys_words)
+        ks_pool = load_scales("ks_pool", keys_scales)
+        q_raw = load_rows("q_raw", query)
+        q2_raw = load_rows("q2_raw", query2)
+        prior_pool = sb.tile([P, T], F32, name="prior_pool", align_bytes=64)
+        nc.sync.dma_start(out=prior_pool[:], in_=prior1)
+        lam_c = column("lam_c")
+        nc.sync.dma_start(out=lam_c[:], in_=lam)
+        vw_pool = load_words("vw_pool", vals_words)
+        vs_pool = load_scales("vs_pool", vals_scales)
+        g_raw = load_rows("g_raw", gout)
+        base_t = wide("base_t")
+        nc.sync.dma_start(out=base_t[:], in_=base)
+
+        kw = gathered("kw", kw_pool, U16)
+        ks = gathered("ks", ks_pool, U8)
+        q_mx = quantised("q", rounded("q_bf", q_raw, True))
+        q2_bf = rounded("q2_bf", q2_raw, True)
+        q2_mx = quantised("q2", q2_bf)
+        a = product("a", q_mx, kw, ks)
+        b = product("b", q2_mx, kw, ks)
+        prior = gathered("prior", prior_pool, F32)
+
+        neg_lam = column("neg_lam")
+        nc.vector.tensor_scalar(neg_lam[:], lam_c[:], -1.0, 0.0, ALU.mult, ALU.add)
+        lam_less_one = column("lam_less_one")
+        nc.vector.tensor_scalar(lam_less_one[:], lam_c[:], 1.0, -1.0, ALU.mult, ALU.add)
+
+        exp_a = wide("exp_a")
+        nc.scalar.activation(exp_a[:], a[:], ACT.Exp)
+        exp_b = wide("exp_b")
+        nc.scalar.activation(exp_b[:], b[:], ACT.Exp)
+        ea = wide("ea")
+        nc.vector.tensor_tensor(ea[:], exp_a[:], prior[:], ALU.mult)
+        neg_eb = wide("neg_eb")
+        nc.vector.scalar_tensor_tensor(neg_eb[:], prior[:], 1.0, exp_b[:], ALU.subtract, ALU.mult)
+        u = wide("u")
+        nc.vector.tensor_tensor(u[:], ea[:], neg_eb[:], ALU.subtract)
+        ln_u = wide("ln_u")
+        nc.scalar.activation(ln_u[:], u[:], ACT.Ln)
+
+        vw = gathered("vw", vw_pool, U16, tag="neg_eb")
+        vs = gathered("vs", vs_pool, U8, tag="vw_pool")
+        g_mx = quantised("g", rounded("g_bf", g_raw, False, tag="vs_pool"))
+        neg_s = wide("neg_s", tag="g_raw")
+        neg_max = column("neg_max")
+        nc.vector.tensor_scalar(neg_s[:], ln_u[:], neg_lam[:], None, ALU.mult, ALU.min, accum_out=neg_max[:])
+        c0 = product("c0", g_mx, vw, vs)
+
+        inv_u = wide("inv_u")
+        nc.scalar.activation(inv_u[:], ln_u[:], ACT.Exp, scale=-1.0)
+        p = wide("p")
+        p_sum = column("p_sum")
+        nc.scalar.activation(p[:], neg_s[:], ACT.Exp, scale=-1.0, bias=neg_max[:], accum_out=p_sum[:])
+        r = wide("r", tag="vs_pool")
+        nc.vector.tensor_tensor(r[:], ea[:], inv_u[:], ALU.mult)
+        h = wide("h")
+        nc.scalar.activation(h[:], r[:], ACT.Identity, scale=lam_less_one[:], bias=1.0)
+        inv_sum = column("inv_sum")
+        nc.vector.reciprocal(inv_sum[:], p_sum[:])
+        pc = wide("pc")
+        pc_sum = column("pc_sum")
+        nc.vector.scalar_tensor_tensor(pc[:], c0[:], 1.0, p[:], ALU.mult, ALU.mult, accum_out=pc_sum[:])
+        lam_w = column("lam_w")
+        nc.vector.tensor_tensor(lam_w[:], lam_c[:], inv_sum[:], ALU.mult)
+        c_mean = column("c_mean")
+        nc.vector.tensor_tensor(c_mean[:], pc_sum[:], inv_sum[:], ALU.mult)
+
+        halves = [slice(0, HALF), slice(HALF, I)]
+        m = wide("m")
+        da = wide("da")
+        for s in halves:
+            nc.vector.scalar_tensor_tensor(m[:, s], r[:, s], lam_w[:], p[:, s], ALU.mult, ALU.mult)
+        for s in halves:
+            nc.vector.scalar_tensor_tensor(da[:, s], c0[:, s], c_mean[:], m[:, s], ALU.subtract, ALU.mult)
+        da_sq = wide("da_sq")
+        sum_sq = column("sum_sq")
+        nc.scalar.activation(da_sq[:], da[:], ACT.Square, accum_out=sum_sq[:])
+        t = wide("t")
+        dm = wide("dm")
+        sum_dm = column("sum_dm")
+        nc.vector.tensor_tensor(t[:, halves[0]], da[:, halves[0]], h[:, halves[0]], ALU.mult)
+        nc.vector.scalar_tensor_tensor(dm[:], da[:], 1.0, m[:], ALU.mult, ALU.mult, accum_out=sum_dm[:])
+        nc.vector.tensor_tensor(t[:, halves[1]], da[:, halves[1]], h[:, halves[1]], ALU.mult)
+        y1 = wide("y1")
+        nw = wide("nw")
+        y = wide("y")
+        for s in halves:
+            nc.vector.scalar_tensor_tensor(y1[:, s], t[:, s], sum_dm[:], da[:, s], ALU.subtract, ALU.mult)
+        for s in halves:
+            nc.vector.scalar_tensor_tensor(nw[:, s], m[:, s], sum_sq[:], y1[:, s], ALU.mult, ALU.subtract)
+        for s in halves:
+            nc.vector.scalar_tensor_tensor(y[:, s], nw[:, s], -PENALTY, base_t[:, s], ALU.mult, ALU.add)
+            nc.sync.dma_start(out=out[:, s], in_=y[:, s])

@@ -20,6 +20,7 @@ P = 128
 PACK = 4
 PENALTY = 512.0 * 2.0 * 512.0
 HALF = I // 2
+LN_FLOOR = 2.0 ** -63
 
 
 def tile_attend_gpeitherquestion_soft_kernel(tc, query, query2, keys_words, keys_scales, prior1, lam, gout, vals_words, vals_scales, base, offs, out):
@@ -51,20 +52,18 @@ def tile_attend_gpeitherquestion_soft_kernel(tc, query, query2, keys_words, keys
             nc.sync.dma_start(out=raw[:], in_=rows.rearrange("(p j) w -> p j w", j=PACK))
             return raw
 
-        def rounded(name, raw, on_scalar, tag=None):
-            grouped = sb.tile([P, Q, PACK], BF16, name=name, tag=tag or name, align_bytes=64)
-            dst = grouped[:].rearrange("p (c i) t -> p c t i", i=4)
+        def rounded(grouped, raw, on_scalar):
+            dst = grouped.rearrange("p (c i) t -> p c t i", i=4)
             src = raw[:].rearrange("p t (c i) -> p c t i", i=4)
             if on_scalar:
                 nc.scalar.activation(dst, src, ACT.Copy)
             else:
                 nc.vector.tensor_copy(dst, src)
-            return grouped
 
-        def quantised(name, grouped):
-            codes = sb.tile([P, Q], U32, name=name + "_codes", align_bytes=64)
-            scales = sb.tile([P, Q], U8, name=name + "_scales", align_bytes=64)
-            nc.vector.quantize_mx(out=codes[:].bitcast(FP8X4), scales=scales[:], in_=grouped[:].rearrange("p w t -> p (w t)"))
+        def quantised(name, grouped, width, tag=None):
+            codes = sb.tile([P, width], U32, name=name + "_codes", tag=tag or name + "_codes", align_bytes=64)
+            scales = sb.tile([P, width], U8, name=name + "_scales", align_bytes=64)
+            nc.vector.quantize_mx(out=codes[:].bitcast(FP8X4), scales=scales[:], in_=grouped)
             return codes, scales
 
         def gathered(name, pool, dtype, tag=None):
@@ -72,105 +71,134 @@ def tile_attend_gpeitherquestion_soft_kernel(tc, query, query2, keys_words, keys
             nc.vector.tensor_copy(picked[:], pool[:].indirect(offsets[:]))
             return picked
 
-        def product(name, stationary, words, scales):
-            acc = ps.tile([P, I], F32, name=name)
-            nc.tensor.matmul_mx(out=acc[:], lhsT=stationary[0][:].bitcast(FP8X4), lhsT_scale=stationary[1][:],
-                                rhs=words[:].bitcast(FP4X4), rhs_scale=scales[:], start=True, stop=True)
-            return acc
+        def product(acc, row_codes, row_scales, words, scales):
+            nc.tensor.matmul_mx(out=acc, lhsT=row_codes.bitcast(FP8X4), lhsT_scale=row_scales,
+                                rhs=words.bitcast(FP4X4), rhs_scale=scales, start=True, stop=True)
 
+        halves = [slice(0, HALF), slice(HALF, I)]
         offsets = sb.tile([P, I // 16], U16, name="offsets")
         nc.sync.dma_start(offsets[:], offs)
+        prior_pool = sb.tile([P, T], F32, name="prior_pool", tag="prior_pool", align_bytes=64)
+        nc.sync.dma_start(out=prior_pool[P - 1:P, :], in_=prior1[0:1, :])
         kw_pool = load_words("kw_pool", keys_words)
         ks_pool = load_scales("ks_pool", keys_scales)
+        nc.vector.memset(prior_pool[0:P - 1, :], 0.0)
         q_raw = load_rows("q_raw", query)
         q2_raw = load_rows("q2_raw", query2)
-        prior_pool = sb.tile([P, T], F32, name="prior_pool", align_bytes=64)
-        nc.sync.dma_start(out=prior_pool[:], in_=prior1)
-        lam_c = column("lam_c")
-        nc.sync.dma_start(out=lam_c[:], in_=lam)
+        g_raw = load_rows("g_raw", gout)
         vw_pool = load_words("vw_pool", vals_words)
         vs_pool = load_scales("vs_pool", vals_scales)
-        g_raw = load_rows("g_raw", gout)
+        lam_c = column("lam_c")
+        nc.sync.dma_start(out=lam_c[:], in_=lam)
         base_t = wide("base_t")
         nc.sync.dma_start(out=base_t[:], in_=base)
+        identity = sb.tile([P, P], F32, name="identity", align_bytes=64)
+        distance = sb.tile([P, P], F32, name="distance", tag="distance", align_bytes=64)
+        nc.gpsimd.iota(distance[:], [[1, P]], base=0, channel_multiplier=-1, allow_small_or_imprecise_dtypes=True)
+        nc.scalar.activation(distance[:], distance[:], ACT.Abs)
+        nc.scalar.activation(identity[:], distance[:], ACT.Relu, scale=-1.0, bias=1.0)
 
+        prior_row = wide("prior_row", tag="distance")
+        nc.scalar.activation(prior_row[:], prior_pool[:].indirect(offsets[:]), ACT.Copy)
+        turned = ps.tile([P, I // P, P], F32, name="turned", tag="turned")
+        for j in range(I // P):
+            nc.tensor.transpose(turned[:, j, :], prior_row[:, j * P:(j + 1) * P], identity[:])
         kw = gathered("kw", kw_pool, U16)
         ks = gathered("ks", ks_pool, U8)
-        q_mx = quantised("q", rounded("q_bf", q_raw, True))
-        q2_bf = rounded("q2_bf", q2_raw, True)
-        q2_mx = quantised("q2", q2_bf)
-        a = product("a", q_mx, kw, ks)
-        b = product("b", q2_mx, kw, ks)
-        prior = gathered("prior", prior_pool, F32)
+        qq_bf = sb.tile([P, 2, Q, PACK], BF16, name="qq_bf", tag="prior_pool", align_bytes=64)
+        rounded(qq_bf[:, 0], q_raw, True)
+        rounded(qq_bf[:, 1], q2_raw, False)
+        prior_cols = sb.tile([P, I // P], F32, name="prior_cols", align_bytes=64)
+        nc.vector.tensor_copy(prior_cols[:], turned[:, :, P - 1])
+        qq_codes, qq_scales = quantised("qq", qq_bf[:].rearrange("p n w t -> p (n w t)"), 2 * Q, tag="distance")
+        g_bf = sb.tile([P, Q, PACK], BF16, name="g_bf", tag="q_raw", align_bytes=64)
+        rounded(g_bf[:], g_raw, True)
+        vw = gathered("vw", vw_pool, U16, tag="prior_pool")
+        g_codes, g_scales = quantised("g", g_bf[:].rearrange("p w t -> p (w t)"), Q)
 
-        neg_lam = column("neg_lam")
-        nc.vector.tensor_scalar(neg_lam[:], lam_c[:], -1.0, 0.0, ALU.mult, ALU.add)
-        lam_less_one = column("lam_less_one")
-        nc.vector.tensor_scalar(lam_less_one[:], lam_c[:], 1.0, -1.0, ALU.mult, ALU.add)
-
-        exp_a = wide("exp_a")
+        a = ps.tile([P, I], F32, name="a")
+        product(a[:], qq_codes[:, 0:Q], qq_scales[:, 0:Q], kw[:], ks[:])
+        b = ps.tile([P, I], F32, name="b")
+        product(b[:], qq_codes[:, Q:2 * Q], qq_scales[:, Q:2 * Q], kw[:], ks[:])
+        prior = ps.tile([P, I], F32, name="prior")
+        for j in range(I // P):
+            nc.tensor.transpose(prior[:, j * P:(j + 1) * P], prior_cols[:, j:j + 1].to_broadcast([P, P]), identity[:])
+        exp_a = wide("exp_a", tag="g_raw")
         nc.scalar.activation(exp_a[:], a[:], ACT.Exp)
         exp_b = wide("exp_b")
         nc.scalar.activation(exp_b[:], b[:], ACT.Exp)
-        ea = wide("ea")
-        nc.vector.tensor_tensor(ea[:], exp_a[:], prior[:], ALU.mult)
-        neg_eb = wide("neg_eb")
-        nc.vector.scalar_tensor_tensor(neg_eb[:], prior[:], 1.0, exp_b[:], ALU.subtract, ALU.mult)
-        u = wide("u")
-        nc.vector.tensor_tensor(u[:], ea[:], neg_eb[:], ALU.subtract)
-        ln_u = wide("ln_u")
-        nc.scalar.activation(ln_u[:], u[:], ACT.Ln)
 
-        vw = gathered("vw", vw_pool, U16, tag="neg_eb")
+        neg_lam = column("neg_lam")
+        nc.gpsimd.tensor_scalar(neg_lam[:], lam_c[:], -1.0, 0.0, ALU.mult, ALU.add)
+        lam_less_one = column("lam_less_one")
+        nc.gpsimd.tensor_scalar(lam_less_one[:], lam_c[:], 1.0, -1.0, ALU.mult, ALU.add)
+
         vs = gathered("vs", vs_pool, U8, tag="vw_pool")
-        g_mx = quantised("g", rounded("g_bf", g_raw, False, tag="vs_pool"))
-        neg_s = wide("neg_s", tag="g_raw")
+        c0 = ps.tile([P, I], F32, name="c0")
+        product(c0[:], g_codes[:], g_scales[:], vw[:], vs[:])
+
+        ea = wide("ea", tag="vs_pool")
+        neg_eb = wide("neg_eb", tag="q_raw")
+        u = wide("u")
+        ln_ea = wide("ln_ea")
+        ln_u = wide("ln_u")
+        nc.vector.tensor_tensor(ea[:], prior[:], exp_a[:], ALU.mult)
+        nc.scalar.activation(ln_ea[:], ea[:], ACT.Ln, bias=LN_FLOOR)
+        for s in halves:
+            nc.vector.scalar_tensor_tensor(neg_eb[:, s], prior[:, s], 1.0, exp_b[:, s], ALU.subtract, ALU.mult)
+        for s in halves:
+            nc.vector.tensor_tensor(u[:, s], ea[:, s], neg_eb[:, s], ALU.subtract)
+            nc.scalar.activation(ln_u[:, s], u[:, s], ACT.Ln)
+
+        neg_s = wide("neg_s")
         neg_max = column("neg_max")
         nc.vector.tensor_scalar(neg_s[:], ln_u[:], neg_lam[:], None, ALU.mult, ALU.min, accum_out=neg_max[:])
-        c0 = product("c0", g_mx, vw, vs)
+        ln_rp = wide("ln_rp")
+        nc.vector.scalar_tensor_tensor(ln_rp[:], ln_u[:], lam_less_one[:], ln_ea[:], ALU.mult, ALU.add)
+        ln_r = wide("ln_r")
+        nc.vector.tensor_tensor(ln_r[:], ln_ea[:], ln_u[:], ALU.subtract)
 
-        inv_u = wide("inv_u")
-        nc.scalar.activation(inv_u[:], ln_u[:], ACT.Exp, scale=-1.0)
         p = wide("p")
         p_sum = column("p_sum")
         nc.scalar.activation(p[:], neg_s[:], ACT.Exp, scale=-1.0, bias=neg_max[:], accum_out=p_sum[:])
-        r = wide("r", tag="vs_pool")
-        nc.vector.tensor_tensor(r[:], ea[:], inv_u[:], ALU.mult)
+        rp = wide("rp", tag="neg_s")
+        nc.scalar.activation(rp[:], ln_rp[:], ACT.Exp, bias=neg_max[:])
+        r = wide("r", tag="ln_rp")
+        nc.scalar.activation(r[:], ln_r[:], ACT.Exp)
         h = wide("h")
         nc.scalar.activation(h[:], r[:], ACT.Identity, scale=lam_less_one[:], bias=1.0)
+
         inv_sum = column("inv_sum")
         nc.vector.reciprocal(inv_sum[:], p_sum[:])
-        pc = wide("pc")
-        pc_sum = column("pc_sum")
-        nc.vector.scalar_tensor_tensor(pc[:], c0[:], 1.0, p[:], ALU.mult, ALU.mult, accum_out=pc_sum[:])
-        lam_w = column("lam_w")
-        nc.vector.tensor_tensor(lam_w[:], lam_c[:], inv_sum[:], ALU.mult)
+        wc = wide("wc")
         c_mean = column("c_mean")
-        nc.vector.tensor_tensor(c_mean[:], pc_sum[:], inv_sum[:], ALU.mult)
+        nc.vector.scalar_tensor_tensor(wc[:], c0[:], inv_sum[:], p[:], ALU.mult, ALU.mult, accum_out=c_mean[:])
+        lam_w = column("lam_w")
+        nc.gpsimd.tensor_tensor(lam_w[:], inv_sum[:], lam_c[:], ALU.mult)
+        factor = column("factor")
+        nc.gpsimd.tensor_scalar(factor[:], lam_w[:], lam_w[:], -PENALTY, ALU.mult, ALU.mult)
 
-        halves = [slice(0, HALF), slice(HALF, I)]
-        m = wide("m")
-        da = wide("da")
+        d = wide("d")
         for s in halves:
-            nc.vector.scalar_tensor_tensor(m[:, s], r[:, s], lam_w[:], p[:, s], ALU.mult, ALU.mult)
-        for s in halves:
-            nc.vector.scalar_tensor_tensor(da[:, s], c0[:, s], c_mean[:], m[:, s], ALU.subtract, ALU.mult)
-        da_sq = wide("da_sq")
+            nc.vector.scalar_tensor_tensor(d[:, s], c0[:, s], c_mean[:], rp[:, s], ALU.subtract, ALU.mult)
+        d_rp = wide("d_rp")
+        sum_d_rp = column("sum_d_rp")
+        nc.vector.scalar_tensor_tensor(d_rp[:], d[:], lam_w[:], rp[:], ALU.mult, ALU.mult, accum_out=sum_d_rp[:])
+        d_sq = wide("d_sq")
         sum_sq = column("sum_sq")
-        nc.scalar.activation(da_sq[:], da[:], ACT.Square, accum_out=sum_sq[:])
-        t = wide("t")
-        dm = wide("dm")
-        sum_dm = column("sum_dm")
-        nc.vector.tensor_tensor(t[:, halves[0]], da[:, halves[0]], h[:, halves[0]], ALU.mult)
-        nc.vector.scalar_tensor_tensor(dm[:], da[:], 1.0, m[:], ALU.mult, ALU.mult, accum_out=sum_dm[:])
-        nc.vector.tensor_tensor(t[:, halves[1]], da[:, halves[1]], h[:, halves[1]], ALU.mult)
+        nc.scalar.activation(d_sq[:], d[:], ACT.Square, accum_out=sum_sq[:])
+        sum_sq_w = column("sum_sq_w")
+        nc.scalar.activation(sum_sq_w[:], sum_sq[:], ACT.Copy, scale=lam_w[:])
+        dh = wide("dh")
         y1 = wide("y1")
         nw = wide("nw")
         y = wide("y")
         for s in halves:
-            nc.vector.scalar_tensor_tensor(y1[:, s], t[:, s], sum_dm[:], da[:, s], ALU.subtract, ALU.mult)
+            nc.vector.tensor_tensor(dh[:, s], d[:, s], h[:, s], ALU.mult)
         for s in halves:
-            nc.vector.scalar_tensor_tensor(nw[:, s], m[:, s], sum_sq[:], y1[:, s], ALU.mult, ALU.subtract)
+            nc.vector.scalar_tensor_tensor(y1[:, s], dh[:, s], sum_d_rp[:], d[:, s], ALU.subtract, ALU.mult)
         for s in halves:
-            nc.vector.scalar_tensor_tensor(y[:, s], nw[:, s], -PENALTY, base_t[:, s], ALU.mult, ALU.add)
+            nc.vector.scalar_tensor_tensor(nw[:, s], rp[:, s], sum_sq_w[:], y1[:, s], ALU.mult, ALU.subtract)
+        for s in halves:
+            nc.vector.scalar_tensor_tensor(y[:, s], nw[:, s], factor[:], base_t[:, s], ALU.mult, ALU.add)
             nc.sync.dma_start(out=out[:, s], in_=y[:, s])

@@ -133,11 +133,7 @@ def tile_attend_gpeitherquestion_soft_kernel(tc, query, query2, keys_words, keys
         lam_less_one = column("lam_less_one")
         nc.gpsimd.tensor_scalar(lam_less_one[:], lam_c[:], 1.0, -1.0, ALU.mult, ALU.add)
 
-        vs = gathered("vs", vs_pool, U8, tag="vw_pool")
-        c0 = ps.tile([P, I], F32, name="c0")
-        product(c0[:], g_codes[:], g_scales[:], vw[:], vs[:])
-
-        ea = wide("ea", tag="vs_pool")
+        ea = wide("ea", tag="vw_pool")
         neg_eb = wide("neg_eb", tag="q_raw")
         u = wide("u")
         ln_ea = wide("ln_ea")
@@ -150,7 +146,11 @@ def tile_attend_gpeitherquestion_soft_kernel(tc, query, query2, keys_words, keys
             nc.vector.tensor_tensor(u[:, s], ea[:, s], neg_eb[:, s], ALU.subtract)
             nc.scalar.activation(ln_u[:, s], u[:, s], ACT.Ln)
 
-        neg_s = wide("neg_s")
+        vs = gathered("vs", vs_pool, U8, tag="q_raw")
+        c0 = ps.tile([P, I], F32, name="c0")
+        product(c0[:], g_codes[:], g_scales[:], vw[:], vs[:])
+
+        neg_s = wide("neg_s", tag="vs_pool")
         neg_max = column("neg_max")
         nc.vector.tensor_scalar(neg_s[:], ln_u[:], neg_lam[:], None, ALU.mult, ALU.min, accum_out=neg_max[:])
         ln_rp = wide("ln_rp")
@@ -161,7 +161,7 @@ def tile_attend_gpeitherquestion_soft_kernel(tc, query, query2, keys_words, keys
         p = wide("p")
         p_sum = column("p_sum")
         nc.scalar.activation(p[:], neg_s[:], ACT.Exp, scale=-1.0, bias=neg_max[:], accum_out=p_sum[:])
-        rp = wide("rp", tag="neg_s")
+        rp = wide("rp", tag="vs_pool")
         nc.scalar.activation(rp[:], ln_rp[:], ACT.Exp, bias=neg_max[:])
         r = wide("r", tag="ln_rp")
         nc.scalar.activation(r[:], ln_r[:], ACT.Exp)

@@ -107,11 +107,11 @@ def tile_attend_gpeitherquestion_soft_kernel(tc, query, query2, keys_words, keys
         ks = gathered("ks", ks_pool, U8)
         qq_bf = sb.tile([P, 2, Q, PACK], BF16, name="qq_bf", tag="prior_pool", align_bytes=64)
         rounded(qq_bf[:, 0], q_raw, True)
-        rounded(qq_bf[:, 1], q2_raw, False)
+        rounded(qq_bf[:, 1], q2_raw, True)
         prior_cols = sb.tile([P, I // P], F32, name="prior_cols", align_bytes=64)
         nc.vector.tensor_copy(prior_cols[:], turned[:, :, P - 1])
         qq_codes, qq_scales = quantised("qq", qq_bf[:].rearrange("p n w t -> p (n w t)"), 2 * Q, tag="distance")
-        g_bf = sb.tile([P, Q, PACK], BF16, name="g_bf", tag="q_raw", align_bytes=64)
+        g_bf = sb.tile([P, Q, PACK], BF16, name="g_bf", tag="q2_raw", align_bytes=64)
         rounded(g_bf[:], g_raw, True)
         vw = gathered("vw", vw_pool, U16, tag="prior_pool")
         g_codes, g_scales = quantised("g", g_bf[:].rearrange("p w t -> p (w t)"), Q)
@@ -134,7 +134,7 @@ def tile_attend_gpeitherquestion_soft_kernel(tc, query, query2, keys_words, keys
         nc.gpsimd.tensor_scalar(lam_less_one[:], lam_c[:], 1.0, -1.0, ALU.mult, ALU.add)
 
         ea = wide("ea", tag="vw_pool")
-        neg_eb = wide("neg_eb", tag="q_raw")
+        neg_eb = wide("neg_eb", tag="q2_raw")
         u = wide("u")
         ln_ea = wide("ln_ea")
         ln_u = wide("ln_u")
@@ -146,7 +146,7 @@ def tile_attend_gpeitherquestion_soft_kernel(tc, query, query2, keys_words, keys
             nc.vector.tensor_tensor(u[:, s], ea[:, s], neg_eb[:, s], ALU.subtract)
             nc.scalar.activation(ln_u[:, s], u[:, s], ACT.Ln)
 
-        vs = gathered("vs", vs_pool, U8, tag="q_raw")
+        vs = gathered("vs", vs_pool, U8, tag="q2_raw")
         c0 = ps.tile([P, I], F32, name="c0")
         product(c0[:], g_codes[:], g_scales[:], vw[:], vs[:])
 

from contextlib import ExitStack

import concourse.mybir as mybir

D, E, T, I, Q = 512, 512, 2048, 512, 128
FLOPS = 3 * 2 * D * Q * I

F32 = mybir.dt.float32
BF16 = mybir.dt.bfloat16
I32 = mybir.dt.int32
U32 = mybir.dt.uint32
U16 = mybir.dt.uint16
U8 = mybir.dt.uint8
FP8X4 = mybir.dt.float8_e4m3fn_x4
FP4X4 = mybir.dt.float4_e2m1fn_x4
ALU = mybir.AluOpType
ACT = mybir.ActivationFunctionType

P = 128
PACK = 4
PENALTY = 512.0 * 2.0 * 512.0
HALF = I // 2
LN_FLOOR = 2.0 ** -63


def tile_attend_gpeitherquestion_soft_kernel(tc, query, query2, keys_words, keys_scales, prior1, lam, gout, vals_words, vals_scales, base, offs, out):
    nc = tc.nc
    with ExitStack() as ctx:
        sb = ctx.enter_context(tc.tile_pool(name="sb", bufs=1))
        ps = ctx.enter_context(tc.psum_pool(name="ps", bufs=1))

        def wide(name, tag=None):
            return sb.tile([P, I], F32, name=name, tag=tag or name, align_bytes=64)

        def column(name):
            return sb.tile([P, 1], F32, name=name)

        def load_words(name, words):
            pool = sb.tile([P, T], U16, name=name, tag=name, align_bytes=64)
            nc.sync.dma_start(out=pool[:].bitcast(I32), in_=words[0].bitcast(I32))
            return pool

        def load_scales(name, scales):
            pool = sb.tile([P, T], U8, name=name, tag=name, align_bytes=64)
            nc.vector.memset(pool[:].bitcast(I32), 0)
            for r in range(PACK):
                nc.sync.dma_start(out=pool[r:P:32, :].bitcast(I32), in_=scales[0][r:16:PACK, :].bitcast(I32))
            return pool

        def load_rows(name, rows):
            raw = sb.tile([P, PACK, Q], F32, name=name, tag=name, align_bytes=64)
            nc.sync.dma_start(out=raw[:], in_=rows.rearrange("(p j) w -> p j w", j=PACK))
            return raw

        def rounded(grouped, raw, on_scalar):
            dst = grouped.rearrange("p (c i) t -> p c t i", i=4)
            src = raw[:].rearrange("p t (c i) -> p c t i", i=4)
            if on_scalar:
                nc.scalar.activation(dst, src, ACT.Copy)
            else:
                nc.vector.tensor_copy(dst, src)

        def quantised(name, grouped, width, tag=None):
            codes = sb.tile([P, width], U32, name=name + "_codes", tag=tag or name + "_codes", align_bytes=64)
            scales = sb.tile([P, width], U8, name=name + "_scales", align_bytes=64)
            nc.vector.quantize_mx(out=codes[:].bitcast(FP8X4), scales=scales[:], in_=grouped)
            return codes, scales

        def gathered(name, pool, dtype, tag=None):
            picked = sb.tile([P, I], dtype, name=name, tag=tag or name, align_bytes=64)
            nc.vector.tensor_copy(picked[:], pool[:].indirect(offsets[:]))
            return picked

        def product(acc, row_codes, row_scales, words, scales):
            nc.tensor.matmul_mx(out=acc, lhsT=row_codes.bitcast(FP8X4), lhsT_scale=row_scales,
                                rhs=words.bitcast(FP4X4), rhs_scale=scales, start=True, stop=True)

        halves = [slice(0, HALF), slice(HALF, I)]
        offsets = sb.tile([P, I // 16], U16, name="offsets")
        nc.sync.dma_start(offsets[:], offs)
        prior_pool = sb.tile([P, T], F32, name="prior_pool", tag="prior_pool", align_bytes=64)
        nc.sync.dma_start(out=prior_pool[P - 1:P, :], in_=prior1[0:1, :])
        kw_pool = load_words("kw_pool", keys_words)
        ks_pool = load_scales("ks_pool", keys_scales)
        nc.vector.memset(prior_pool[0:P - 1, :], 0.0)
        q_raw = load_rows("q_raw", query)
        q2_raw = load_rows("q2_raw", query2)
        g_raw = load_rows("g_raw", gout)
        vw_pool = load_words("vw_pool", vals_words)
        vs_pool = load_scales("vs_pool", vals_scales)
        lam_c = column("lam_c")
        nc.sync.dma_start(out=lam_c[:], in_=lam)
        base_t = wide("base_t")
        nc.sync.dma_start(out=base_t[:], in_=base)
        identity = sb.tile([P, P], F32, name="identity", align_bytes=64)
        distance = sb.tile([P, P], F32, name="distance", tag="distance", align_bytes=64)
        nc.gpsimd.iota(distance[:], [[1, P]], base=0, channel_multiplier=-1, allow_small_or_imprecise_dtypes=True)
        nc.scalar.activation(distance[:], distance[:], ACT.Abs)
        nc.scalar.activation(identity[:], distance[:], ACT.Relu, scale=-1.0, bias=1.0)

        prior_row = wide("prior_row", tag="distance")
        nc.scalar.activation(prior_row[:], prior_pool[:].indirect(offsets[:]), ACT.Copy)
        turned = ps.tile([P, I // P, P], F32, name="turned", tag="turned")
        for j in range(I // P):
            nc.tensor.transpose(turned[:, j, :], prior_row[:, j * P:(j + 1) * P], identity[:])
        kw = gathered("kw", kw_pool, U16)
        ks = gathered("ks", ks_pool, U8)
        qq_bf = sb.tile([P, 2, Q, PACK], BF16, name="qq_bf", tag="prior_pool", align_bytes=64)
        rounded(qq_bf[:, 0], q_raw, True)
        rounded(qq_bf[:, 1], q2_raw, True)
        prior_cols = sb.tile([P, I // P], F32, name="prior_cols", align_bytes=64)
        nc.vector.tensor_copy(prior_cols[:], turned[:, :, P - 1])
        qq_codes, qq_scales = quantised("qq", qq_bf[:].rearrange("p n w t -> p (n w t)"), 2 * Q, tag="distance")
        g_bf = sb.tile([P, Q, PACK], BF16, name="g_bf", tag="q2_raw", align_bytes=64)
        rounded(g_bf[:], g_raw, True)
        vw = gathered("vw", vw_pool, U16, tag="prior_pool")
        g_codes, g_scales = quantised("g", g_bf[:].rearrange("p w t -> p (w t)"), Q)

        a = ps.tile([P, I], F32, name="a")
        product(a[:], qq_codes[:, 0:Q], qq_scales[:, 0:Q], kw[:], ks[:])
        b = ps.tile([P, I], F32, name="b")
        product(b[:], qq_codes[:, Q:2 * Q], qq_scales[:, Q:2 * Q], kw[:], ks[:])
        prior = ps.tile([P, I], F32, name="prior")
        for j in range(I // P):
            nc.tensor.transpose(prior[:, j * P:(j + 1) * P], prior_cols[:, j:j + 1].to_broadcast([P, P]), identity[:])
        exp_a = wide("exp_a", tag="g_raw")
        nc.scalar.activation(exp_a[:], a[:], ACT.Exp)
        exp_b = wide("exp_b")
        nc.scalar.activation(exp_b[:], b[:], ACT.Exp)

        neg_lam = column("neg_lam")
        nc.gpsimd.tensor_scalar(neg_lam[:], lam_c[:], -1.0, 0.0, ALU.mult, ALU.add)
        lam_less_one = column("lam_less_one")
        nc.gpsimd.tensor_scalar(lam_less_one[:], lam_c[:], 1.0, -1.0, ALU.mult, ALU.add)

        ea = wide("ea", tag="vw_pool")
        neg_eb = wide("neg_eb", tag="q2_raw")
        u = wide("u")
        ln_ea = wide("ln_ea")
        ln_u = wide("ln_u")
        nc.vector.tensor_tensor(ea[:], prior[:], exp_a[:], ALU.mult)
        nc.scalar.activation(ln_ea[:], ea[:], ACT.Ln, bias=LN_FLOOR)
        for s in halves:
            nc.vector.scalar_tensor_tensor(neg_eb[:, s], prior[:, s], 1.0, exp_b[:, s], ALU.subtract, ALU.mult)
        for s in halves:
            nc.vector.tensor_tensor(u[:, s], ea[:, s], neg_eb[:, s], ALU.subtract)
            nc.scalar.activation(ln_u[:, s], u[:, s], ACT.Ln)

        vs = gathered("vs", vs_pool, U8, tag="q2_raw")
        c0 = ps.tile([P, I], F32, name="c0")
        product(c0[:], g_codes[:], g_scales[:], vw[:], vs[:])

        neg_s = wide("neg_s", tag="vs_pool")
        neg_max = column("neg_max")
        nc.vector.tensor_scalar(neg_s[:], ln_u[:], neg_lam[:], None, ALU.mult, ALU.min, accum_out=neg_max[:])
        ln_rp = wide("ln_rp")
        nc.vector.scalar_tensor_tensor(ln_rp[:], ln_u[:], lam_less_one[:], ln_ea[:], ALU.mult, ALU.add)
        ln_r = wide("ln_r")
        nc.vector.tensor_tensor(ln_r[:], ln_ea[:], ln_u[:], ALU.subtract)

        p = wide("p")
        p_sum = column("p_sum")
        nc.scalar.activation(p[:], neg_s[:], ACT.Exp, scale=-1.0, bias=neg_max[:], accum_out=p_sum[:])
        rp = wide("rp", tag="vs_pool")
        nc.scalar.activation(rp[:], ln_rp[:], ACT.Exp, bias=neg_max[:])
        r = wide("r", tag="ln_rp")
        nc.scalar.activation(r[:], ln_r[:], ACT.Exp)
        h = wide("h")
        nc.scalar.activation(h[:], r[:], ACT.Identity, scale=lam_less_one[:], bias=1.0)

        inv_sum = column("inv_sum")
        nc.vector.reciprocal(inv_sum[:], p_sum[:])
        wc = wide("wc")
        c_mean = column("c_mean")
        nc.vector.scalar_tensor_tensor(wc[:], c0[:], inv_sum[:], p[:], ALU.mult, ALU.mult, accum_out=c_mean[:])
        lam_w = column("lam_w")
        nc.gpsimd.tensor_tensor(lam_w[:], inv_sum[:], lam_c[:], ALU.mult)
        factor = column("factor")
        nc.gpsimd.tensor_scalar(factor[:], lam_w[:], lam_w[:], -PENALTY, ALU.mult, ALU.mult)

        d = wide("d")
        for s in halves:
            nc.vector.scalar_tensor_tensor(d[:, s], c0[:, s], c_mean[:], rp[:, s], ALU.subtract, ALU.mult)
        d_rp = wide("d_rp")
        sum_d_rp = column("sum_d_rp")
        nc.vector.scalar_tensor_tensor(d_rp[:], d[:], lam_w[:], rp[:], ALU.mult, ALU.mult, accum_out=sum_d_rp[:])
        d_sq = wide("d_sq")
        sum_sq = column("sum_sq")
        nc.scalar.activation(d_sq[:], d[:], ACT.Square, accum_out=sum_sq[:])
        sum_sq_w = column("sum_sq_w")
        nc.scalar.activation(sum_sq_w[:], sum_sq[:], ACT.Copy, scale=lam_w[:])
        dh = wide("dh")
        y1 = wide("y1")
        nw = wide("nw")
        y = wide("y")
        for s in halves:
            nc.vector.tensor_tensor(dh[:, s], d[:, s], h[:, s], ALU.mult)
        for s in halves:
            nc.vector.scalar_tensor_tensor(y1[:, s], dh[:, s], sum_d_rp[:], d[:, s], ALU.subtract, ALU.mult)
        for s in halves:
            nc.vector.scalar_tensor_tensor(nw[:, s], rp[:, s], sum_sq_w[:], y1[:, s], ALU.mult, ALU.subtract)
        for s in halves:
            nc.vector.scalar_tensor_tensor(y[:, s], nw[:, s], factor[:], base_t[:, s], ALU.mult, ALU.add)
            nc.sync.dma_start(out=out[:, s], in_=y[:, s])
